import numpy as np
import ml_dtypes


def mxq(x, axis, fmt="e4m3"):
    dtype, down = {"e4m3": (ml_dtypes.float8_e4m3fn, 7), "e5m2": (ml_dtypes.float8_e5m2, 14)}[fmt]
    v = np.moveaxis(np.asarray(x, np.float32).astype(ml_dtypes.bfloat16).astype(np.float64), axis, -1)
    blocks = v.reshape(v.shape[:-1] + (-1, 32))
    amax = np.abs(blocks).max(-1, keepdims=True)
    byte = np.maximum(np.where(amax > 0, np.frexp(amax)[1] - 1 + 127, 0) - down, 1)
    scale = np.exp2(byte - 127.0)
    codes = (blocks / scale).astype(np.float32).astype(dtype).astype(np.float64)
    return np.moveaxis((codes * scale).reshape(v.shape), -1, axis)


WIDE = False


def mx_kscale(k):
    if not WIDE:
        return np.ones(k)
    levels = np.array([10, -10, 5, -5, 0])
    if k % 512:
        return np.exp2(np.random.permutation(np.resize(levels, k // 32))).repeat(32)
    a = np.empty((k // 512, 16))
    for p in range(k // 512):
        a[p, :8] = np.random.permutation(np.resize(levels, 8))
        for g in range(8):
            far = levels[np.abs(levels - a[p, g]) >= 10]
            a[p, g + 8] = far[np.random.randint(len(far))]
    return np.exp2(a.ravel()).repeat(32)


def f64(x):
    return np.asarray(x).astype(np.float64)


def striped(idx):
    return np.tile(idx.reshape(-1, 16).T, (8, 1)).astype(np.uint16)


def unstriped(offs):
    return offs[:16].T.reshape(-1).astype(np.int64)


E2M1 = np.array([0.0, 0.5, 1.0, 1.5, 2.0, 3.0, 4.0, 6.0, -0.0, -0.5, -1.0, -1.5, -2.0, -3.0, -4.0, -6.0])


def pack_weight(w, fmt):
    k, n = w.shape
    w = f64(np.asarray(w, np.float32).astype(ml_dtypes.bfloat16)).reshape(k // 32, 32, n)
    amax = np.abs(w).max(1)
    if fmt == "e4m3":
        byte = np.frexp(amax)[1] - 1 + 127 - 7
    else:
        mant, ex = np.frexp(amax / 6.0)
        byte = np.where(mant > 0.5, ex, ex - 1) + 127
    byte = np.clip(np.where(amax > 0, byte, 1), 1, 254)
    scaled = (w * np.exp2(127.0 - byte)[:, None, :]).reshape(k, n).astype(np.float32)
    by_word = np.ascontiguousarray(scaled.reshape(k // 512, 128, 4, n).transpose(0, 1, 3, 2))
    if fmt == "e4m3":
        words = by_word.astype(ml_dtypes.float8_e4m3fn).view(np.uint8)
    else:
        c = by_word.astype(ml_dtypes.float4_e2m1fn).view(np.uint8) & 0xF
        words = (c[..., 0::2] | (c[..., 1::2] << 4)).reshape(k // 512, 128, 2 * n)
    return np.ascontiguousarray(words), np.ascontiguousarray(byte.astype(np.uint8).reshape(k // 512, 16, n))


def unpack_weight(words, scales, fmt):
    g, _, n = scales.shape
    words = np.ascontiguousarray(words).reshape(g, 128, n, -1)
    if fmt == "e4m3":
        vals = words.view(ml_dtypes.float8_e4m3fn).astype(np.float64)
    else:
        nib = np.empty((g, 128, n, 4), np.uint8)
        nib[..., 0::2] = words & 0xF
        nib[..., 1::2] = words >> 4
        vals = E2M1[nib]
    vals = vals * np.repeat(np.exp2(scales.astype(np.float64) - 127.0), 8, axis=1)[..., None]
    return vals.transpose(0, 1, 3, 2).reshape(g * 512, n)


def gelu(v):
    return 0.5 * v * (1.0 + np.tanh(np.sqrt(2.0 / np.pi) * (v + 0.044715 * v**3)))


def bf(x):
    return np.asarray(x, np.float32).astype(ml_dtypes.bfloat16)


def planes(Y):
    n, m = Y.shape
    b = f64(bf(Y)).reshape(n // 32, 32, m)
    amax = np.abs(b).max(1)
    byte = np.clip(np.where(amax > 0, np.frexp(amax)[1] - 1 + 127 - 7, 1), 1, 254)
    codes = (b * np.exp2(127.0 - byte)[:, None, :]).reshape(n, m).astype(np.float32).astype(ml_dtypes.float8_e4m3fn).view(np.uint8)
    words = codes.reshape(n // 512, 128, 4, m).transpose(0, 1, 3, 2)
    return np.ascontiguousarray(words), np.ascontiguousarray(byte.astype(np.uint8).reshape(n // 512, 16, m))


T, S, P, K, H, N = 4096, 1024, 512, 1024, 1024, 1024


def setup_inputs():
    n = np.random.standard_normal
    s = mx_kscale(K)[:, None]
    u = mx_kscale(H)[:, None]
    size = np.exp(0.8 * n(N))[None, :]
    d = {}
    d["tab_words"], d["tab_scales"] = pack_weight(n((K, T)) * s, "e2m1")
    d["offs"] = striped(np.random.permutation(T)[:S])
    d["w1"] = (n((K, H)) / K**0.5 / s).astype(np.float32)
    d["gain"] = (np.exp(0.3 * n(H)) * u[:, 0]).astype(np.float32)
    d["pos1"] = striped(np.random.permutation(S)[:P])
    d["pos2"] = striped(np.random.permutation(S)[:P])
    d["tint"] = (1.3 * np.exp(0.3 * n(H)) / u[:, 0]).astype(np.float32)
    d["b3"] = (0.7 * n(H)).astype(np.float32)
    d["lift"] = (np.exp(0.3 * n(H)) * u[:, 0]).astype(np.float32)
    d["w2"] = (n((H, N)) / H**0.5 / u * size).astype(np.float32)
    d["w3_words"], d["w3_scales"] = pack_weight(n((H, N)) / H**0.5 / u * size, "e2m1")
    return d


def reference(tab_words, tab_scales, offs, w1, gain, pos1, pos2, tint, b3, lift, w2, w3_words, w3_scales):
    v = unpack_weight(tab_words, tab_scales, "e2m1")[:, unstriped(offs)]
    w3 = unpack_weight(w3_words, w3_scales, "e2m1")
    h = f64(gain)[:, None] * (mxq(f64(w1), 0, "e4m3").T @ v)
    hs = mxq(h[:, unstriped(pos1)], 0, "e4m3")
    a = f64(tint)[:, None] * h[:, unstriped(pos2)] + f64(b3)[:, None]
    x = 0.5 * a * (1.0 + np.tanh(0.7978845608028654 * (a + 0.044715 * a * a * a)))
    x = mxq(f64(lift)[:, None] * x, 0, "e4m3")
    y = mxq(f64(w2), 0, "e4m3").T @ hs + w3.T @ x
    words, scales = planes(y)
    return y, words, scales

@@ -1,0 +1,347 @@
+from contextlib import ExitStack
+
+import concourse.mybir as mybir
+
+T, S, PAIRS, K, H, N = 4096, 1024, 512, 1024, 1024, 1024
+FLOPS = 2 * K * H * S + 2 * 2 * H * N * PAIRS
+
+F32 = mybir.dt.float32
+BF16 = mybir.dt.bfloat16
+I32 = mybir.dt.int32
+U32 = mybir.dt.uint32
+U16 = mybir.dt.uint16
+U8 = mybir.dt.uint8
+FP8X4 = mybir.dt.float8_e4m3fn_x4
+FP4X4 = mybir.dt.float4_e2m1fn_x4
+ACT = mybir.ActivationFunctionType
+ALU = mybir.AluOpType
+
+P = 128
+PACK = 4
+PASS = P * PACK
+BANK = 512
+HALF = PAIRS // 2
+
+
+def tile_list_neighbouring_pane_features_kernel(
+    tc, tab_words, tab_scales, offs, w1, gain, pos1, pos2, tint, b3, lift, w2, w3_words, w3_scales, out_0, out_1, out_2
+):
+    nc = tc.nc
+    with ExitStack() as ctx:
+        lists = ctx.enter_context(tc.tile_pool(name="lists", bufs=1))
+        keep = ctx.enter_context(tc.tile_pool(name="keep", bufs=1))
+        ring = ctx.enter_context(tc.tile_pool(name="ring", bufs=1))
+        psum = ctx.enter_context(tc.psum_pool(name="psum", bufs=1))
+
+        def held(name, shape, dtype):
+            return keep.tile(shape, dtype, name=name, align_bytes=64)
+
+        def bank(i, shape):
+            return psum.tile(shape, F32, name="bank%d" % i)
+
+        offs_t = lists.tile([P, S // 16], U16, name="offs_t")
+        pos1_t = lists.tile([P, PAIRS // 16], U16, name="pos1_t")
+        pos2_t = lists.tile([P, PAIRS // 16], U16, name="pos2_t")
+
+        tab_sc = held("tab_sc", [P, T], U8)
+        nc.vector.memset(tab_sc[:].bitcast(I32), 0)
+        w3_sc_raw = held("w3_sc_raw", [P, 2, N], U8)
+        nc.vector.memset(w3_sc_raw[:].rearrange("p b n -> p (b n)").bitcast(I32), 0)
+        v_sc1 = held("v_sc1", [P, S], U8)
+        nc.vector.memset(v_sc1[:].bitcast(I32), 0)
+
+        warm = held("warm", [P, 8], F32)
+        nc.vector.memset(warm[:], 0.0)
+        warm_out = held("warm_out", [P, 8], F32)
+        nc.scalar.activation(warm_out[:], warm[:], ACT.Gelu_apprx_tanh)
+
+        nc.sync.dma_start(offs_t[:], offs)
+        nc.sync.dma_start(pos2_t[:], pos2)
+        nc.sync.dma_start(pos1_t[:], pos1)
+        rows = {}
+        for name, vec in (("gain", gain), ("tint", tint), ("b3", b3), ("lift", lift)):
+            rows[name] = held("row_" + name, [P, 2, PACK], F32)
+            nc.sync.dma_start(out=rows[name][:], in_=vec.rearrange("(b p t) -> p b t", p=P, t=PACK))
+        tab_w = [held("tab_w0", [P, T], U16)]
+        nc.sync.dma_start(out=tab_w[0][:].bitcast(I32), in_=tab_words[0].bitcast(I32))
+        for q in range(4):
+            nc.sync.dma_start(
+                out=tab_sc[32 * q : 32 * q + 8, :].bitcast(I32),
+                in_=tab_scales[:, 4 * q : 4 * q + 4, :].bitcast(I32),
+            )
+        for q in range(4):
+            nc.gpsimd.dma_start(
+                out=w3_sc_raw[32 * q : 32 * q + 4, :, :].bitcast(I32),
+                in_=w3_scales[:, 4 * q : 4 * q + 4, :].bitcast(I32).rearrange("b r n -> r b n"),
+            )
+
+        def load_weight(w, a, g, c0, c1, tag, bufs):
+            raw = ring.tile([P, PACK, c1 - c0], F32, name=tag, bufs=bufs)
+            src = w[a * PASS : (a + 1) * PASS, g * PASS + c0 : g * PASS + c1]
+            nc.sync.dma_start(out=raw[:], in_=src.rearrange("(p j) c -> p j c", j=PACK))
+            return raw
+
+        def load_halves(w, a, g):
+            return [load_weight(w, a, g, u * 256, (u + 1) * 256, "raw_half", 2) for u in range(2)]
+
+        w1_raw = {}
+        w1_raw[0, 0] = load_weight(w1, 0, 0, 0, PASS, "raw", 2)
+        tab_w.append(ring.tile([P, T], U16, name="raw", bufs=2))
+        nc.sync.dma_start(out=tab_w[1][:].bitcast(I32), in_=tab_words[1].bitcast(I32))
+        w1_last = load_halves(w1, 1, 0)
+        w3_raw = ring.tile([P, 2, 2 * N], U8, name="raw_half", bufs=2)
+        nc.sync.dma_start(out=w3_raw[:].bitcast(I32), in_=w3_words.bitcast(I32).rearrange("b p n -> p b n"))
+
+        def deal_cast(copy, grouped, raw, m0, m1):
+            copy(
+                grouped[:, :, m0:m1, :].rearrange("p t m j -> p m j t"),
+                raw[:].rearrange("p j (m t) -> p m j t", t=PACK),
+            )
+
+        def new_grouped():
+            return ring.tile([P, PACK, P, PACK], BF16, name="w_grouped", bufs=5, align_bytes=64)
+
+        def quantize(codes, scales, grouped_flat):
+            nc.vector.quantize_mx(out=codes.bitcast(FP8X4), scales=scales, in_=grouped_flat)
+
+        w_codes, w_scales = {}, {}
+
+        def quantize_weight(key, grouped, pieces):
+            w_codes[key] = held("wc_%s_%d_%d" % key, [P, PASS], U32)
+            w_scales[key] = held("ws_%s_%d_%d" % key, [P, PASS], U8)
+            flat = grouped[:].rearrange("p t m j -> p (t m j)")
+            step = PASS // pieces
+            for i in range(pieces):
+                cols = slice(i * step, (i + 1) * step)
+                quantize(w_codes[key][:, cols], w_scales[key][:, cols], flat[:, PACK * i * step : PACK * (i + 1) * step])
+
+        v_sc0 = held("v_sc0", [P, S], U8)
+        nc.vector.tensor_copy(v_sc0[:], tab_sc[:].indirect(offs_t[:]))
+        for q in range(4):
+            nc.sync.dma_start(
+                out=v_sc1[32 * q : 32 * q + 4, :].bitcast(I32), in_=v_sc0[32 * q + 4 : 32 * q + 8, :].bitcast(I32)
+            )
+        v_sc = [v_sc0, v_sc1]
+        v_w = [held("v_w%d" % a, [P, S], U16) for a in range(2)]
+        nc.vector.tensor_copy(v_w[0][:], tab_w[0][:].indirect(offs_t[:]))
+
+        grouped = new_grouped()
+        deal_cast(nc.scalar.copy, grouped, w1_raw[0, 0], 0, P)
+        quantize_weight(("w1", 0, 0), grouped, 1)
+        nc.vector.tensor_copy(v_w[1][:], tab_w[1][:].indirect(offs_t[:]))
+
+        h_banks = {}
+
+        def first_pass(a, b, t, u):
+            if a == 0:
+                h_banks[b, t, u] = bank(2 * t + u, [P, BANK])
+            key = ("w1", a, b)
+            cols = slice(u * BANK, (u + 1) * BANK)
+            nc.tensor.matmul_mx(
+                out=h_banks[b, t, u][:],
+                lhsT=w_codes[key][:, t * P : (t + 1) * P].bitcast(FP8X4),
+                lhsT_scale=w_scales[key][:, t * P : (t + 1) * P],
+                rhs=v_w[a][:, cols].bitcast(FP4X4),
+                rhs_scale=v_sc[a][:, cols],
+                start=(a == 0),
+                stop=(a == 1),
+            )
+
+        grouped = new_grouped()
+        deal_cast(nc.scalar.copy, grouped, w1_last[0], 0, P // 2)
+        deal_cast(nc.scalar.copy, grouped, w1_last[1], P // 2, P)
+        quantize_weight(("w1", 1, 0), grouped, 2)
+        for t in range(PACK):
+            for a in range(2):
+                for u in range(2):
+                    first_pass(a, 0, t, u)
+
+        for a in range(2):
+            w1_raw[a, 1] = load_weight(w1, a, 1, 0, PASS, "raw", 2)
+        w2_raw = {}
+        w2_raw[0, 0] = load_halves(w2, 0, 0)
+        w2_raw[0, 1] = load_weight(w2, 0, 1, 0, PASS, "raw", 2)
+        w2_raw[1, 0] = load_weight(w2, 1, 0, 0, PASS, "raw", 2)
+        w2_raw[1, 1] = load_halves(w2, 1, 1)
+
+        h = {}
+
+        def empty_h(b, t):
+            h[b, t] = held("h_%d_%d" % (b, t), [P, S], F32)
+            scale = rows["gain"][:, b, t : t + 1]
+            for u in range(2):
+                nc.scalar.activation(h[b, t][:, u * BANK : (u + 1) * BANK], h_banks[b, t, u][:], ACT.Copy, scale=scale)
+
+        picked2, hs_rows, x_rows = {}, {}, {}
+
+        def pick1(piece, t):
+            b, m0, m1 = piece
+            nc.vector.tensor_copy(hs_rows[piece][:, t, :], h[b, t][:].indirect(pos1_t[:, m0 // 16 : m1 // 16]))
+
+        def pick2(piece, t):
+            b, m0, m1 = piece
+            nc.vector.tensor_copy(picked2[piece, t], h[b, t][:].indirect(pos2_t[:, m0 // 16 : m1 // 16]))
+
+        def gelu_lift(piece, t):
+            b, m0, m1 = piece
+            bent = ring.tile([P, m1 - m0], F32, name="bent", bufs=2)
+            nc.scalar.activation(
+                bent[:], picked2[piece, t], ACT.Gelu_apprx_tanh,
+                bias=rows["b3"][:, b, t : t + 1], scale=rows["tint"][:, b, t : t + 1],
+            )
+            nc.scalar.activation(x_rows[piece][:, t, :], bent[:], ACT.Copy, scale=rows["lift"][:, b, t : t + 1])
+
+        act_codes = {(n, b): held("%s_codes%d" % (n, b), [P, PAIRS], U32) for n in ("hs", "x") for b in range(2)}
+        act_scales = {(n, b): held("%s_scales%d" % (n, b), [P, PAIRS], U8) for n in ("hs", "x") for b in range(2)}
+
+        def interleave(copy, src):
+            width = src.shape[2]
+            woven = ring.tile([P, width, PACK], BF16, name="woven", bufs=4, align_bytes=64)
+            copy(woven[:].rearrange("p (c i) t -> p c t i", i=4), src.rearrange("p t (c i) -> p c t i", i=4))
+            return woven[:].rearrange("p m t -> p (m t)")
+
+        def quantize_act(name, b, woven, m0, m1):
+            quantize(act_codes[name, b][:, m0:m1], act_scales[name, b][:, m0:m1], woven)
+
+        def cast_weight(raw, copy):
+            grouped = new_grouped()
+            if isinstance(raw, list):
+                for u in range(2):
+                    deal_cast(copy, grouped, raw[u], u * P // 2, (u + 1) * P // 2)
+            else:
+                deal_cast(copy, grouped, raw, 0, P)
+            return grouped
+
+        y_banks = {}
+
+        def second(name, b, u):
+            for g in range(2):
+                for c in range(2 * u, 2 * u + 2):
+                    first = (g, c) not in y_banks
+                    if first:
+                        y_banks[g, c] = bank(2 * c + g, [P, PACK, P])
+                    for t in range(PACK):
+                        if name == "x":
+                            n0 = g * PASS + t * P
+                            words, scale = w3_w[:, b, n0 : n0 + P].bitcast(FP4X4), w3_sc[:, b, n0 : n0 + P]
+                        else:
+                            key = ("w2", b, g)
+                            words, scale = w_codes[key][:, t * P : (t + 1) * P].bitcast(FP8X4), w_scales[key][:, t * P : (t + 1) * P]
+                        nc.tensor.matmul_mx(
+                            out=y_banks[g, c][:, t, :],
+                            lhsT=words,
+                            lhsT_scale=scale,
+                            rhs=act_codes[name, b][:, c * P : (c + 1) * P].bitcast(FP8X4),
+                            rhs_scale=act_scales[name, b][:, c * P : (c + 1) * P],
+                            start=(first and t == 0),
+                            stop=(name == "hs" and b == 1 and t == PACK - 1),
+                        )
+
+        y_codes = held("y_codes", [P, 2, PAIRS], U32)
+        y_scales = held("y_scales", [P, 2, PAIRS], U8)
+
+        def finish(u, g, from_psum):
+            cols = slice(u * HALF, (u + 1) * HALF)
+            y = ring.tile([P, PACK, HALF], F32, name="y", bufs=4)
+            for i in range(2):
+                nc.scalar.copy(y[:, :, i * P : (i + 1) * P], y_banks[g, 2 * u + i][:])
+            nc.sync.dma_start(
+                out=out_0[g * PASS : (g + 1) * PASS, cols].rearrange("(p t) m -> p t m", t=PACK), in_=y[:]
+            )
+            if from_psum:
+                woven = ring.tile([P, HALF, PACK], BF16, name="woven", bufs=4, align_bytes=64)
+                for i in range(2):
+                    nc.scalar.copy(woven[:, i * P : (i + 1) * P, :], y_banks[g, 2 * u + i][:].rearrange("p t m -> p m t"))
+                woven = woven[:].rearrange("p m t -> p (m t)")
+            else:
+                woven = interleave(nc.vector.tensor_copy, y[:])
+            quantize(y_codes[:, g, cols], y_scales[:, g, cols], woven)
+            nc.sync.dma_start(
+                out=out_1[g].rearrange("p m t -> p (m t)").bitcast(I32)[:, cols], in_=y_codes[:, g, cols].bitcast(I32)
+            )
+
+        for a in range(2):
+            quantize_weight(("w1", a, 1), cast_weight(w1_raw[a, 1], nc.vector.tensor_copy), 1)
+        for t in range(PACK):
+            empty_h(0, t)
+        for t in range(PACK):
+            for a in range(2):
+                for u in range(2):
+                    first_pass(a, 1, t, u)
+            empty_h(1, t)
+        whole, early, late = (0, 0, PAIRS), (1, 0, HALF), (1, HALF, PAIRS)
+
+        def rows_tile(tag, piece, dtype):
+            return ring.tile([P, PACK, piece[2] - piece[1]], dtype, name=tag, bufs=1)
+
+        def weave_quantize(name, piece, copy):
+            src = hs_rows[piece] if name == "hs" else x_rows[piece]
+            quantize_act(name, piece[0], interleave(copy, src[:]), piece[1], piece[2])
+
+        hs_rows[whole] = rows_tile("rows_a", whole, BF16)
+        x_rows[whole] = rows_tile("rows_b", whole, BF16)
+        for t in range(PACK):
+            picked2[whole, t] = ring.tile([P, PAIRS], F32, name="picked", bufs=4)[:]
+            pick2(whole, t)
+            pick1(whole, t)
+        w3_w = held("w3_w", [P, 2, N], U16)
+        nc.vector.tensor_copy(
+            w3_w[:].rearrange("p b (g t m) -> p (b g) t m", t=PACK, m=P),
+            w3_raw[:].bitcast(U16).rearrange("p b (g m t) -> p (b g) t m", t=PACK, m=P),
+        )
+        w3_sc = held("w3_sc", [P, 2, N], U8)
+        nc.vector.tensor_copy(
+            w3_sc[:].rearrange("p b (g t m) -> p (b g) t m", t=PACK, m=P),
+            w3_sc_raw[:].rearrange("p b (g m t) -> p (b g) t m", t=PACK, m=P),
+        )
+        weave_quantize("hs", whole, nc.vector.tensor_copy)
+        quantize_weight(("w2", 0, 0), cast_weight(w2_raw[0, 0], nc.scalar.copy), 1)
+        for t in range(PACK):
+            gelu_lift(whole, t)
+        weave_quantize("x", whole, nc.scalar.copy)
+        for u in range(2):
+            second("x", 0, u)
+        quantize_weight(("w2", 0, 1), cast_weight(w2_raw[0, 1], nc.scalar.copy), 1)
+        for u in range(2):
+            second("hs", 0, u)
+
+        for g in range(2):
+            quantize_weight(("w2", 1, g), cast_weight(w2_raw[1, g], nc.scalar.copy), 1)
+        hs_rows[early] = rows_tile("rows_a", early, BF16)
+        x_rows[early] = rows_tile("rows_c", early, BF16)
+        for t in range(PACK):
+            picked2[early, t] = ring.tile([P, HALF], F32, name="picked", bufs=4)[:]
+            pick2(early, t)
+        for t in range(PACK):
+            pick1(early, t)
+        for t in range(PACK):
+            gelu_lift(early, t)
+        weave_quantize("hs", early, nc.vector.tensor_copy)
+        weave_quantize("x", early, nc.vector.tensor_copy)
+        second("x", 1, 0)
+        second("hs", 1, 0)
+
+        late_picked = rows_tile("rows_b", late, F32)
+        hs_rows[late] = rows_tile("rows_c", late, BF16)
+        x_rows[late] = rows_tile("rows_d", late, BF16)
+        for t in range(PACK):
+            picked2[late, t] = late_picked[:, t, :]
+            pick2(late, t)
+        for t in range(PACK):
+            gelu_lift(late, t)
+        for t in range(PACK):
+            pick1(late, t)
+        weave_quantize("x", late, nc.vector.tensor_copy)
+        weave_quantize("hs", late, nc.vector.tensor_copy)
+        second("x", 1, 1)
+        second("hs", 1, 1)
+        for g in range(2):
+            finish(0, g, g == 0)
+        for g in range(2):
+            finish(1, g, False)
+        for q in range(4):
+            queue = nc.sync if q % 2 == 0 else nc.scalar
+            queue.dma_start(
+                out=out_2[:, 4 * q : 4 * q + 4, :].bitcast(I32).rearrange("g r m -> r g m"),
+                in_=y_scales[32 * q : 32 * q + 4, :, :].bitcast(I32),
+            )

@@ -45,8 +45,6 @@ def tile_list_neighbouring_pane_features_kernel(
 
         tab_sc = held("tab_sc", [P, T], U8)
         nc.vector.memset(tab_sc[:].bitcast(I32), 0)
-        w3_sc_raw = held("w3_sc_raw", [P, 2, N], U8)
-        nc.vector.memset(w3_sc_raw[:].rearrange("p b n -> p (b n)").bitcast(I32), 0)
         v_sc1 = held("v_sc1", [P, S], U8)
         nc.vector.memset(v_sc1[:].bitcast(I32), 0)
 
@@ -62,18 +60,6 @@ def tile_list_neighbouring_pane_features_kernel(
         for name, vec in (("gain", gain), ("tint", tint), ("b3", b3), ("lift", lift)):
             rows[name] = held("row_" + name, [P, 2, PACK], F32)
             nc.sync.dma_start(out=rows[name][:], in_=vec.rearrange("(b p t) -> p b t", p=P, t=PACK))
-        tab_w = [held("tab_w0", [P, T], U16)]
-        nc.sync.dma_start(out=tab_w[0][:].bitcast(I32), in_=tab_words[0].bitcast(I32))
-        for q in range(4):
-            nc.sync.dma_start(
-                out=tab_sc[32 * q : 32 * q + 8, :].bitcast(I32),
-                in_=tab_scales[:, 4 * q : 4 * q + 4, :].bitcast(I32),
-            )
-        for q in range(4):
-            nc.gpsimd.dma_start(
-                out=w3_sc_raw[32 * q : 32 * q + 4, :, :].bitcast(I32),
-                in_=w3_scales[:, 4 * q : 4 * q + 4, :].bitcast(I32).rearrange("b r n -> r b n"),
-            )
 
         def load_weight(w, a, g, c0, c1, tag, bufs):
             raw = ring.tile([P, PACK, c1 - c0], F32, name=tag, bufs=bufs)
@@ -81,16 +67,22 @@ def tile_list_neighbouring_pane_features_kernel(
             nc.sync.dma_start(out=raw[:], in_=src.rearrange("(p j) c -> p j c", j=PACK))
             return raw
 
+        w1_raw = {}
+        w1_raw[0, 0] = load_weight(w1, 0, 0, 0, PASS, "raw_first", 1)
+        for q in range(4):
+            nc.sync.dma_start(
+                out=tab_sc[32 * q : 32 * q + 8, :].bitcast(I32),
+                in_=tab_scales[:, 4 * q : 4 * q + 4, :].bitcast(I32),
+            )
+
         def load_halves(w, a, g):
             return [load_weight(w, a, g, u * 256, (u + 1) * 256, "raw_half", 2) for u in range(2)]
 
-        w1_raw = {}
-        w1_raw[0, 0] = load_weight(w1, 0, 0, 0, PASS, "raw", 2)
-        tab_w.append(ring.tile([P, T], U16, name="raw", bufs=2))
-        nc.sync.dma_start(out=tab_w[1][:].bitcast(I32), in_=tab_words[1].bitcast(I32))
-        w1_last = load_halves(w1, 1, 0)
-        w3_raw = ring.tile([P, 2, 2 * N], U8, name="raw_half", bufs=2)
-        nc.sync.dma_start(out=w3_raw[:].bitcast(I32), in_=w3_words.bitcast(I32).rearrange("b p n -> p b n"))
+        tab_w, w1_last = [], []
+        for a in range(2):
+            tab_w.append(ring.tile([P, T], U16, name="raw", bufs=2))
+            nc.sync.dma_start(out=tab_w[a][:].bitcast(I32), in_=tab_words[a].bitcast(I32))
+            w1_last.append(load_weight(w1, 1, 0, a * 256, (a + 1) * 256, "raw_half", 2))
 
         def deal_cast(copy, grouped, raw, m0, m1):
             copy(
@@ -99,7 +91,7 @@ def tile_list_neighbouring_pane_features_kernel(
             )
 
         def new_grouped():
-            return ring.tile([P, PACK, P, PACK], BF16, name="w_grouped", bufs=5, align_bytes=64)
+            return ring.tile([P, PACK, P, PACK], BF16, name="w_grouped", bufs=4, align_bytes=64)
 
         def quantize(codes, scales, grouped_flat):
             nc.vector.quantize_mx(out=codes.bitcast(FP8X4), scales=scales, in_=grouped_flat)
@@ -158,10 +150,12 @@ def tile_list_neighbouring_pane_features_kernel(
 
         for a in range(2):
             w1_raw[a, 1] = load_weight(w1, a, 1, 0, PASS, "raw", 2)
+        w3_raw = ring.tile([P, 2, 2 * N], U8, name="raw_half", bufs=2)
+        nc.sync.dma_start(out=w3_raw[:].bitcast(I32), in_=w3_words.bitcast(I32).rearrange("b p n -> p b n"))
         w2_raw = {}
         w2_raw[0, 0] = load_halves(w2, 0, 0)
-        w2_raw[0, 1] = load_weight(w2, 0, 1, 0, PASS, "raw", 2)
         w2_raw[1, 0] = load_weight(w2, 1, 0, 0, PASS, "raw", 2)
+        w2_raw[0, 1] = load_weight(w2, 0, 1, 0, PASS, "raw", 2)
         w2_raw[1, 1] = load_halves(w2, 1, 1)
 
         h = {}
@@ -203,8 +197,9 @@ def tile_list_neighbouring_pane_features_kernel(
         def quantize_act(name, b, woven, m0, m1):
             quantize(act_codes[name, b][:, m0:m1], act_scales[name, b][:, m0:m1], woven)
 
-        def cast_weight(raw, copy):
-            grouped = new_grouped()
+        def cast_weight(raw, copy, grouped=None):
+            if grouped is None:
+                grouped = new_grouped()
             if isinstance(raw, list):
                 for u in range(2):
                     deal_cast(copy, grouped, raw[u], u * P // 2, (u + 1) * P // 2)
@@ -214,9 +209,9 @@ def tile_list_neighbouring_pane_features_kernel(
 
         y_banks = {}
 
-        def second(name, b, u):
-            for g in range(2):
-                for c in range(2 * u, 2 * u + 2):
+        def second(names, b, u, g):
+            for c in range(2 * u, 2 * u + 2):
+                for name in names:
                     first = (g, c) not in y_banks
                     if first:
                         y_banks[g, c] = bank(2 * c + g, [P, PACK, P])
@@ -260,10 +255,11 @@ def tile_list_neighbouring_pane_features_kernel(
                 out=out_1[g].rearrange("p m t -> p (m t)").bitcast(I32)[:, cols], in_=y_codes[:, g, cols].bitcast(I32)
             )
 
-        for a in range(2):
-            quantize_weight(("w1", a, 1), cast_weight(w1_raw[a, 1], nc.vector.tensor_copy), 1)
+        quantize_weight(("w1", 0, 1), cast_weight(w1_raw[0, 1], nc.vector.tensor_copy), 1)
         for t in range(PACK):
             empty_h(0, t)
+        grouped = ring.tile([P, PACK, P, PACK], BF16, name="rows_a", bufs=1, align_bytes=64)
+        quantize_weight(("w1", 1, 1), cast_weight(w1_raw[1, 1], nc.scalar.copy, grouped), 1)
         for t in range(PACK):
             for a in range(2):
                 for u in range(2):
@@ -272,18 +268,27 @@ def tile_list_neighbouring_pane_features_kernel(
         whole, early, late = (0, 0, PAIRS), (1, 0, HALF), (1, HALF, PAIRS)
 
         def rows_tile(tag, piece, dtype):
-            return ring.tile([P, PACK, piece[2] - piece[1]], dtype, name=tag, bufs=1)
+            return ring.tile([P, PACK, piece[2] - piece[1]], dtype, name=tag, bufs=1, align_bytes=64)
 
         def weave_quantize(name, piece, copy):
             src = hs_rows[piece] if name == "hs" else x_rows[piece]
             quantize_act(name, piece[0], interleave(copy, src[:]), piece[1], piece[2])
 
-        hs_rows[whole] = rows_tile("rows_a", whole, BF16)
+        hs_rows[whole] = ring.tile([P, PACK, PAIRS], BF16, name="rows_a", bufs=1, align_bytes=64)
         x_rows[whole] = rows_tile("rows_b", whole, BF16)
         for t in range(PACK):
             picked2[whole, t] = ring.tile([P, PAIRS], F32, name="picked", bufs=4)[:]
             pick2(whole, t)
             pick1(whole, t)
+        weave_quantize("hs", whole, nc.vector.tensor_copy)
+        quantize_weight(("w2", 0, 0), cast_weight(w2_raw[0, 0], nc.scalar.copy), 1)
+        w3_sc_raw = ring.tile([P, 2, N], U8, name="w_grouped", bufs=4, align_bytes=64)
+        nc.vector.memset(w3_sc_raw[:].rearrange("p b n -> p (b n)").bitcast(I32), 0)
+        for q in range(4):
+            nc.sync.dma_start(
+                out=w3_sc_raw[32 * q : 32 * q + 4, :, :].bitcast(I32),
+                in_=w3_scales[:, 4 * q : 4 * q + 4, :].bitcast(I32).rearrange("b r n -> r b n"),
+            )
         w3_w = held("w3_w", [P, 2, N], U16)
         nc.vector.tensor_copy(
             w3_w[:].rearrange("p b (g t m) -> p (b g) t m", t=PACK, m=P),
@@ -294,19 +299,12 @@ def tile_list_neighbouring_pane_features_kernel(
             w3_sc[:].rearrange("p b (g t m) -> p (b g) t m", t=PACK, m=P),
             w3_sc_raw[:].rearrange("p b (g m t) -> p (b g) t m", t=PACK, m=P),
         )
-        weave_quantize("hs", whole, nc.vector.tensor_copy)
-        quantize_weight(("w2", 0, 0), cast_weight(w2_raw[0, 0], nc.scalar.copy), 1)
         for t in range(PACK):
             gelu_lift(whole, t)
         weave_quantize("x", whole, nc.scalar.copy)
-        for u in range(2):
-            second("x", 0, u)
-        quantize_weight(("w2", 0, 1), cast_weight(w2_raw[0, 1], nc.scalar.copy), 1)
-        for u in range(2):
-            second("hs", 0, u)
+        quantize_weight(("w2", 1, 0), cast_weight(w2_raw[1, 0], nc.scalar.copy), 1)
+        second(("x", "hs"), 0, 0, 0)
 
-        for g in range(2):
-            quantize_weight(("w2", 1, g), cast_weight(w2_raw[1, g], nc.scalar.copy), 1)
         hs_rows[early] = rows_tile("rows_a", early, BF16)
         x_rows[early] = rows_tile("rows_c", early, BF16)
         for t in range(PACK):
@@ -318,8 +316,12 @@ def tile_list_neighbouring_pane_features_kernel(
             gelu_lift(early, t)
         weave_quantize("hs", early, nc.vector.tensor_copy)
         weave_quantize("x", early, nc.vector.tensor_copy)
-        second("x", 1, 0)
-        second("hs", 1, 0)
+        second(("x", "hs"), 1, 0, 0)
+        second(("x", "hs"), 0, 1, 0)
+        for b in range(2):
+            quantize_weight(("w2", b, 1), cast_weight(w2_raw[b, 1], nc.scalar.copy), 1)
+            second(("x", "hs"), b, 0, 1)
+        second(("x", "hs"), 0, 1, 1)
 
         late_picked = rows_tile("rows_b", late, F32)
         hs_rows[late] = rows_tile("rows_c", late, BF16)
@@ -329,14 +331,14 @@ def tile_list_neighbouring_pane_features_kernel(
             pick2(late, t)
         for t in range(PACK):
             gelu_lift(late, t)
+        finish(0, 0, False)
+        finish(0, 1, False)
         for t in range(PACK):
             pick1(late, t)
         weave_quantize("x", late, nc.vector.tensor_copy)
         weave_quantize("hs", late, nc.vector.tensor_copy)
-        second("x", 1, 1)
-        second("hs", 1, 1)
         for g in range(2):
-            finish(0, g, g == 0)
+            second(("x", "hs"), 1, 1, g)
         for g in range(2):
             finish(1, g, False)
         for q in range(4):

@@ -44,9 +44,10 @@ def tile_list_neighbouring_pane_features_kernel(
         pos2_t = lists.tile([P, PAIRS // 16], U16, name="pos2_t")
 
         tab_sc = held("tab_sc", [P, T], U8)
-        nc.vector.memset(tab_sc[:].bitcast(I32), 0)
-        v_sc1 = held("v_sc1", [P, S], U8)
-        nc.vector.memset(v_sc1[:].bitcast(I32), 0)
+        nc.vector.memset(tab_sc[:, : T // 2].bitcast(I32), 0)
+        nc.gpsimd.memset(tab_sc[:, T // 2 :].bitcast(I32), 0)
+        v_sc1 = ring.tile([P, S], U8, name="plane", bufs=1, align_bytes=64)
+        nc.gpsimd.memset(v_sc1[:].bitcast(I32), 0)
 
         warm = held("warm", [P, 8], F32)
         nc.vector.memset(warm[:], 0.0)
@@ -68,7 +69,8 @@ def tile_list_neighbouring_pane_features_kernel(
             return raw
 
         w1_raw = {}
-        w1_raw[0, 0] = load_weight(w1, 0, 0, 0, PASS, "raw_first", 1)
+        tab_w = [held("tab_w0", [P, T], U16)]
+        nc.sync.dma_start(out=tab_w[0][:].bitcast(I32), in_=tab_words[0].bitcast(I32))
         for q in range(4):
             nc.sync.dma_start(
                 out=tab_sc[32 * q : 32 * q + 8, :].bitcast(I32),
@@ -78,17 +80,27 @@ def tile_list_neighbouring_pane_features_kernel(
         def load_halves(w, a, g):
             return [load_weight(w, a, g, u * 256, (u + 1) * 256, "raw_half", 2) for u in range(2)]
 
-        tab_w, w1_last = [], []
-        for a in range(2):
-            tab_w.append(ring.tile([P, T], U16, name="raw", bufs=2))
-            nc.sync.dma_start(out=tab_w[a][:].bitcast(I32), in_=tab_words[a].bitcast(I32))
-            w1_last.append(load_weight(w1, 1, 0, a * 256, (a + 1) * 256, "raw_half", 2))
+        w1_raw[0, 0] = load_weight(w1, 0, 0, 0, PASS, "raw", 2)
+        w1_last = [load_weight(w1, 1, 0, 0, 256, "raw_half", 2)]
+        tab_w.append(ring.tile([P, T], U16, name="raw", bufs=2))
+        nc.sync.dma_start(out=tab_w[1][:].bitcast(I32), in_=tab_words[1].bitcast(I32))
+        w1_last.append(load_weight(w1, 1, 0, 256, 512, "raw_half", 2))
 
         def deal_cast(copy, grouped, raw, m0, m1):
+            if copy is None:
+                return pool_cast(grouped, raw, m0, m1)
             copy(
                 grouped[:, :, m0:m1, :].rearrange("p t m j -> p m j t"),
                 raw[:].rearrange("p j (m t) -> p m j t", t=PACK),
             )
+
+        def pool_cast(grouped, raw, m0, m1):
+            for lo in range(m0, m1, 32):
+                nc.gpsimd.tensor_scalar(
+                    grouped[:, :, lo : lo + 32, :].rearrange("p t m j -> p m t j"),
+                    raw[:, :, PACK * (lo - m0) : PACK * (lo - m0 + 32)].rearrange("p j (m t) -> p m t j", t=PACK),
+                    1.0, 0.0, ALU.mult, ALU.add,
+                )
 
         def new_grouped():
             return ring.tile([P, PACK, P, PACK], BF16, name="w_grouped", bufs=4, align_bytes=64)
@@ -114,7 +126,7 @@ def tile_list_neighbouring_pane_features_kernel(
                 out=v_sc1[32 * q : 32 * q + 4, :].bitcast(I32), in_=v_sc0[32 * q + 4 : 32 * q + 8, :].bitcast(I32)
             )
         v_sc = [v_sc0, v_sc1]
-        v_w = [held("v_w%d" % a, [P, S], U16) for a in range(2)]
+        v_w = [ring.tile([P, S], U16, name="words%d" % a, bufs=1, align_bytes=64) for a in range(2)]
         nc.vector.tensor_copy(v_w[0][:], tab_w[0][:].indirect(offs_t[:]))
 
         grouped = new_grouped()
@@ -153,10 +165,9 @@ def tile_list_neighbouring_pane_features_kernel(
         w3_raw = ring.tile([P, 2, 2 * N], U8, name="raw_half", bufs=2)
         nc.sync.dma_start(out=w3_raw[:].bitcast(I32), in_=w3_words.bitcast(I32).rearrange("b p n -> p b n"))
         w2_raw = {}
-        w2_raw[0, 0] = load_halves(w2, 0, 0)
-        w2_raw[1, 0] = load_weight(w2, 1, 0, 0, PASS, "raw", 2)
-        w2_raw[0, 1] = load_weight(w2, 0, 1, 0, PASS, "raw", 2)
-        w2_raw[1, 1] = load_halves(w2, 1, 1)
+        for g in range(2):
+            for b in range(2):
+                w2_raw[b, g] = load_weight(w2, b, g, 0, PASS, "raw", 2)
 
         h = {}
 
@@ -218,7 +229,7 @@ def tile_list_neighbouring_pane_features_kernel(
                     for t in range(PACK):
                         if name == "x":
                             n0 = g * PASS + t * P
-                            words, scale = w3_w[:, b, n0 : n0 + P].bitcast(FP4X4), w3_sc[:, b, n0 : n0 + P]
+                            words, scale = w3_w[:, b, n0 : n0 + P].bitcast(FP4X4), w3_sc[b][:, n0 : n0 + P]
                         else:
                             key = ("w2", b, g)
                             words, scale = w_codes[key][:, t * P : (t + 1) * P].bitcast(FP8X4), w_scales[key][:, t * P : (t + 1) * P]
@@ -282,23 +293,28 @@ def tile_list_neighbouring_pane_features_kernel(
             pick1(whole, t)
         weave_quantize("hs", whole, nc.vector.tensor_copy)
         quantize_weight(("w2", 0, 0), cast_weight(w2_raw[0, 0], nc.scalar.copy), 1)
-        w3_sc_raw = ring.tile([P, 2, N], U8, name="w_grouped", bufs=4, align_bytes=64)
-        nc.vector.memset(w3_sc_raw[:].rearrange("p b n -> p (b n)").bitcast(I32), 0)
+        w3_sc_raw = ring.tile([P, N], U8, name="w_grouped", bufs=4, align_bytes=64)
+        nc.gpsimd.memset(w3_sc_raw[:].bitcast(I32), 0)
         for q in range(4):
             nc.sync.dma_start(
-                out=w3_sc_raw[32 * q : 32 * q + 4, :, :].bitcast(I32),
-                in_=w3_scales[:, 4 * q : 4 * q + 4, :].bitcast(I32).rearrange("b r n -> r b n"),
+                out=w3_sc_raw[32 * q : 32 * q + 8, :].bitcast(I32),
+                in_=w3_scales[:, 4 * q : 4 * q + 4, :].bitcast(I32),
             )
-        w3_w = held("w3_w", [P, 2, N], U16)
+        w3_w = ring.tile([P, 2, N], U16, name="words1", bufs=1, align_bytes=64)
         nc.vector.tensor_copy(
             w3_w[:].rearrange("p b (g t m) -> p (b g) t m", t=PACK, m=P),
             w3_raw[:].bitcast(U16).rearrange("p b (g m t) -> p (b g) t m", t=PACK, m=P),
         )
-        w3_sc = held("w3_sc", [P, 2, N], U8)
+        w3_sc = [ring.tile([P, N], U8, name="plane", bufs=1, align_bytes=64), held("w3_sc1", [P, N], U8)]
+        nc.gpsimd.memset(w3_sc[1][:].bitcast(I32), 0)
         nc.vector.tensor_copy(
-            w3_sc[:].rearrange("p b (g t m) -> p (b g) t m", t=PACK, m=P),
-            w3_sc_raw[:].rearrange("p b (g m t) -> p (b g) t m", t=PACK, m=P),
+            w3_sc[0][:].rearrange("p (g t m) -> p g t m", t=PACK, m=P),
+            w3_sc_raw[:].rearrange("p (g m t) -> p g t m", t=PACK, m=P),
         )
+        for q in range(4):
+            nc.sync.dma_start(
+                out=w3_sc[1][32 * q : 32 * q + 4, :].bitcast(I32), in_=w3_sc[0][32 * q + 4 : 32 * q + 8, :].bitcast(I32)
+            )
         for t in range(PACK):
             gelu_lift(whole, t)
         weave_quantize("x", whole, nc.scalar.copy)
@@ -315,7 +331,7 @@ def tile_list_neighbouring_pane_features_kernel(
         for t in range(PACK):
             gelu_lift(early, t)
         weave_quantize("hs", early, nc.vector.tensor_copy)
-        weave_quantize("x", early, nc.vector.tensor_copy)
+        weave_quantize("x", early, nc.scalar.copy)
         second(("x", "hs"), 1, 0, 0)
         second(("x", "hs"), 0, 1, 0)
         for b in range(2):
@@ -331,11 +347,11 @@ def tile_list_neighbouring_pane_features_kernel(
             pick2(late, t)
         for t in range(PACK):
             gelu_lift(late, t)
+        weave_quantize("x", late, nc.vector.tensor_copy)
         finish(0, 0, False)
         finish(0, 1, False)
         for t in range(PACK):
             pick1(late, t)
-        weave_quantize("x", late, nc.vector.tensor_copy)
         weave_quantize("hs", late, nc.vector.tensor_copy)
         for g in range(2):
             second(("x", "hs"), 1, 1, g)

from contextlib import ExitStack

import concourse.mybir as mybir

T, S, PAIRS, K, H, N = 4096, 1024, 512, 1024, 1024, 1024
FLOPS = 2 * K * H * S + 2 * 2 * H * N * PAIRS

F32 = mybir.dt.float32
BF16 = mybir.dt.bfloat16
I32 = mybir.dt.int32
U32 = mybir.dt.uint32
U16 = mybir.dt.uint16
U8 = mybir.dt.uint8
FP8X4 = mybir.dt.float8_e4m3fn_x4
FP4X4 = mybir.dt.float4_e2m1fn_x4
ACT = mybir.ActivationFunctionType
ALU = mybir.AluOpType

P = 128
PACK = 4
PASS = P * PACK
BANK = 512
HALF = PAIRS // 2


def tile_list_neighbouring_pane_features_kernel(
    tc, tab_words, tab_scales, offs, w1, gain, pos1, pos2, tint, b3, lift, w2, w3_words, w3_scales, out_0, out_1, out_2
):
    nc = tc.nc
    with ExitStack() as ctx:
        lists = ctx.enter_context(tc.tile_pool(name="lists", bufs=1))
        keep = ctx.enter_context(tc.tile_pool(name="keep", bufs=1))
        ring = ctx.enter_context(tc.tile_pool(name="ring", bufs=1))
        psum = ctx.enter_context(tc.psum_pool(name="psum", bufs=1))

        def held(name, shape, dtype):
            return keep.tile(shape, dtype, name=name, align_bytes=64)

        def bank(i, shape):
            return psum.tile(shape, F32, name="bank%d" % i)

        offs_t = lists.tile([P, S // 16], U16, name="offs_t")
        pos1_t = lists.tile([P, PAIRS // 16], U16, name="pos1_t")
        pos2_t = lists.tile([P, PAIRS // 16], U16, name="pos2_t")

        tab_sc = held("tab_sc", [P, T], U8)
        nc.vector.memset(tab_sc[:, : T // 2].bitcast(I32), 0)
        nc.gpsimd.memset(tab_sc[:, T // 2 :].bitcast(I32), 0)
        v_sc1 = ring.tile([P, S], U8, name="plane", bufs=1, align_bytes=64)
        nc.gpsimd.memset(v_sc1[:].bitcast(I32), 0)

        warm = held("warm", [P, 8], F32)
        nc.vector.memset(warm[:], 0.0)
        warm_out = held("warm_out", [P, 8], F32)
        nc.scalar.activation(warm_out[:], warm[:], ACT.Gelu_apprx_tanh)

        nc.sync.dma_start(offs_t[:], offs)
        nc.sync.dma_start(pos2_t[:], pos2)
        nc.sync.dma_start(pos1_t[:], pos1)
        rows = {}
        for name, vec in (("gain", gain), ("tint", tint), ("b3", b3), ("lift", lift)):
            rows[name] = held("row_" + name, [P, 2, PACK], F32)
            nc.sync.dma_start(out=rows[name][:], in_=vec.rearrange("(b p t) -> p b t", p=P, t=PACK))

        def load_weight(w, a, g, c0, c1, tag, bufs):
            raw = ring.tile([P, PACK, c1 - c0], F32, name=tag, bufs=bufs)
            src = w[a * PASS : (a + 1) * PASS, g * PASS + c0 : g * PASS + c1]
            nc.sync.dma_start(out=raw[:], in_=src.rearrange("(p j) c -> p j c", j=PACK))
            return raw

        w1_raw = {}
        tab_w = [held("tab_w0", [P, T], U16)]
        nc.sync.dma_start(out=tab_w[0][:].bitcast(I32), in_=tab_words[0].bitcast(I32))
        for q in range(4):
            nc.sync.dma_start(
                out=tab_sc[32 * q : 32 * q + 8, :].bitcast(I32),
                in_=tab_scales[:, 4 * q : 4 * q + 4, :].bitcast(I32),
            )

        def load_halves(w, a, g):
            return [load_weight(w, a, g, u * 256, (u + 1) * 256, "raw_half", 2) for u in range(2)]

        w1_raw[0, 0] = load_weight(w1, 0, 0, 0, PASS, "raw", 2)
        w1_last = [load_weight(w1, 1, 0, 0, 256, "raw_half", 2)]
        tab_w.append(ring.tile([P, T], U16, name="raw", bufs=2))
        nc.sync.dma_start(out=tab_w[1][:].bitcast(I32), in_=tab_words[1].bitcast(I32))
        w1_last.append(load_weight(w1, 1, 0, 256, 512, "raw_half", 2))

        def deal_cast(copy, grouped, raw, m0, m1):
            if copy is None:
                return pool_cast(grouped, raw, m0, m1)
            copy(
                grouped[:, :, m0:m1, :].rearrange("p t m j -> p m j t"),
                raw[:].rearrange("p j (m t) -> p m j t", t=PACK),
            )

        def pool_cast(grouped, raw, m0, m1):
            for lo in range(m0, m1, 32):
                nc.gpsimd.tensor_scalar(
                    grouped[:, :, lo : lo + 32, :].rearrange("p t m j -> p m t j"),
                    raw[:, :, PACK * (lo - m0) : PACK * (lo - m0 + 32)].rearrange("p j (m t) -> p m t j", t=PACK),
                    1.0, 0.0, ALU.mult, ALU.add,
                )

        def new_grouped():
            return ring.tile([P, PACK, P, PACK], BF16, name="w_grouped", bufs=4, align_bytes=64)

        def quantize(codes, scales, grouped_flat):
            nc.vector.quantize_mx(out=codes.bitcast(FP8X4), scales=scales, in_=grouped_flat)

        w_codes, w_scales = {}, {}

        def quantize_weight(key, grouped, pieces):
            w_codes[key] = held("wc_%s_%d_%d" % key, [P, PASS], U32)
            w_scales[key] = held("ws_%s_%d_%d" % key, [P, PASS], U8)
            flat = grouped[:].rearrange("p t m j -> p (t m j)")
            step = PASS // pieces
            for i in range(pieces):
                cols = slice(i * step, (i + 1) * step)
                quantize(w_codes[key][:, cols], w_scales[key][:, cols], flat[:, PACK * i * step : PACK * (i + 1) * step])

        v_sc0 = held("v_sc0", [P, S], U8)
        nc.vector.tensor_copy(v_sc0[:], tab_sc[:].indirect(offs_t[:]))
        for q in range(4):
            nc.sync.dma_start(
                out=v_sc1[32 * q : 32 * q + 4, :].bitcast(I32), in_=v_sc0[32 * q + 4 : 32 * q + 8, :].bitcast(I32)
            )
        v_sc = [v_sc0, v_sc1]
        v_w = [ring.tile([P, S], U16, name="words%d" % a, bufs=1, align_bytes=64) for a in range(2)]
        nc.vector.tensor_copy(v_w[0][:], tab_w[0][:].indirect(offs_t[:]))

        grouped = new_grouped()
        deal_cast(nc.scalar.copy, grouped, w1_raw[0, 0], 0, P)
        quantize_weight(("w1", 0, 0), grouped, 1)
        nc.vector.tensor_copy(v_w[1][:], tab_w[1][:].indirect(offs_t[:]))

        h_banks = {}

        def first_pass(a, b, t, u):
            if a == 0:
                h_banks[b, t, u] = bank(2 * t + u, [P, BANK])
            key = ("w1", a, b)
            cols = slice(u * BANK, (u + 1) * BANK)
            nc.tensor.matmul_mx(
                out=h_banks[b, t, u][:],
                lhsT=w_codes[key][:, t * P : (t + 1) * P].bitcast(FP8X4),
                lhsT_scale=w_scales[key][:, t * P : (t + 1) * P],
                rhs=v_w[a][:, cols].bitcast(FP4X4),
                rhs_scale=v_sc[a][:, cols],
                start=(a == 0),
                stop=(a == 1),
            )

        grouped = new_grouped()
        deal_cast(nc.scalar.copy, grouped, w1_last[0], 0, P // 2)
        deal_cast(nc.scalar.copy, grouped, w1_last[1], P // 2, P)
        quantize_weight(("w1", 1, 0), grouped, 2)
        for t in range(PACK):
            for a in range(2):
                for u in range(2):
                    first_pass(a, 0, t, u)

        for a in range(2):
            w1_raw[a, 1] = load_weight(w1, a, 1, 0, PASS, "raw", 2)
        w3_raw = ring.tile([P, 2, 2 * N], U8, name="raw_half", bufs=2)
        nc.sync.dma_start(out=w3_raw[:].bitcast(I32), in_=w3_words.bitcast(I32).rearrange("b p n -> p b n"))
        w2_raw = {}
        for g in range(2):
            for b in range(2):
                w2_raw[b, g] = load_weight(w2, b, g, 0, PASS, "raw", 2)

        h = {}

        def empty_h(b, t):
            h[b, t] = held("h_%d_%d" % (b, t), [P, S], F32)
            scale = rows["gain"][:, b, t : t + 1]
            for u in range(2):
                nc.scalar.activation(h[b, t][:, u * BANK : (u + 1) * BANK], h_banks[b, t, u][:], ACT.Copy, scale=scale)

        picked2, hs_rows, x_rows = {}, {}, {}

        def pick1(piece, t):
            b, m0, m1 = piece
            nc.vector.tensor_copy(hs_rows[piece][:, t, :], h[b, t][:].indirect(pos1_t[:, m0 // 16 : m1 // 16]))

        def pick2(piece, t):
            b, m0, m1 = piece
            nc.vector.tensor_copy(picked2[piece, t], h[b, t][:].indirect(pos2_t[:, m0 // 16 : m1 // 16]))

        def gelu_lift(piece, t):
            b, m0, m1 = piece
            bent = ring.tile([P, m1 - m0], F32, name="bent", bufs=2)
            nc.scalar.activation(
                bent[:], picked2[piece, t], ACT.Gelu_apprx_tanh,
                bias=rows["b3"][:, b, t : t + 1], scale=rows["tint"][:, b, t : t + 1],
            )
            nc.scalar.activation(x_rows[piece][:, t, :], bent[:], ACT.Copy, scale=rows["lift"][:, b, t : t + 1])

        act_codes = {(n, b): held("%s_codes%d" % (n, b), [P, PAIRS], U32) for n in ("hs", "x") for b in range(2)}
        act_scales = {(n, b): held("%s_scales%d" % (n, b), [P, PAIRS], U8) for n in ("hs", "x") for b in range(2)}

        def interleave(copy, src):
            width = src.shape[2]
            woven = ring.tile([P, width, PACK], BF16, name="woven", bufs=4, align_bytes=64)
            copy(woven[:].rearrange("p (c i) t -> p c t i", i=4), src.rearrange("p t (c i) -> p c t i", i=4))
            return woven[:].rearrange("p m t -> p (m t)")

        def quantize_act(name, b, woven, m0, m1):
            quantize(act_codes[name, b][:, m0:m1], act_scales[name, b][:, m0:m1], woven)

        def cast_weight(raw, copy, grouped=None):
            if grouped is None:
                grouped = new_grouped()
            if isinstance(raw, list):
                for u in range(2):
                    deal_cast(copy, grouped, raw[u], u * P // 2, (u + 1) * P // 2)
            else:
                deal_cast(copy, grouped, raw, 0, P)
            return grouped

        y_banks = {}

        def second(names, b, u, g):
            for c in range(2 * u, 2 * u + 2):
                for name in names:
                    first = (g, c) not in y_banks
                    if first:
                        y_banks[g, c] = bank(2 * c + g, [P, PACK, P])
                    for t in range(PACK):
                        if name == "x":
                            n0 = g * PASS + t * P
                            words, scale = w3_w[:, b, n0 : n0 + P].bitcast(FP4X4), w3_sc[b][:, n0 : n0 + P]
                        else:
                            key = ("w2", b, g)
                            words, scale = w_codes[key][:, t * P : (t + 1) * P].bitcast(FP8X4), w_scales[key][:, t * P : (t + 1) * P]
                        nc.tensor.matmul_mx(
                            out=y_banks[g, c][:, t, :],
                            lhsT=words,
                            lhsT_scale=scale,
                            rhs=act_codes[name, b][:, c * P : (c + 1) * P].bitcast(FP8X4),
                            rhs_scale=act_scales[name, b][:, c * P : (c + 1) * P],
                            start=(first and t == 0),
                            stop=(name == "hs" and b == 1 and t == PACK - 1),
                        )

        y_codes = held("y_codes", [P, 2, PAIRS], U32)
        y_scales = held("y_scales", [P, 2, PAIRS], U8)

        def finish(u, g, from_psum):
            cols = slice(u * HALF, (u + 1) * HALF)
            y = ring.tile([P, PACK, HALF], F32, name="y", bufs=4)
            for i in range(2):
                nc.scalar.copy(y[:, :, i * P : (i + 1) * P], y_banks[g, 2 * u + i][:])
            nc.sync.dma_start(
                out=out_0[g * PASS : (g + 1) * PASS, cols].rearrange("(p t) m -> p t m", t=PACK), in_=y[:]
            )
            if from_psum:
                woven = ring.tile([P, HALF, PACK], BF16, name="woven", bufs=4, align_bytes=64)
                for i in range(2):
                    nc.scalar.copy(woven[:, i * P : (i + 1) * P, :], y_banks[g, 2 * u + i][:].rearrange("p t m -> p m t"))
                woven = woven[:].rearrange("p m t -> p (m t)")
            else:
                woven = interleave(nc.vector.tensor_copy, y[:])
            quantize(y_codes[:, g, cols], y_scales[:, g, cols], woven)
            nc.sync.dma_start(
                out=out_1[g].rearrange("p m t -> p (m t)").bitcast(I32)[:, cols], in_=y_codes[:, g, cols].bitcast(I32)
            )

        quantize_weight(("w1", 0, 1), cast_weight(w1_raw[0, 1], nc.vector.tensor_copy), 1)
        for t in range(PACK):
            empty_h(0, t)
        grouped = ring.tile([P, PACK, P, PACK], BF16, name="rows_a", bufs=1, align_bytes=64)
        quantize_weight(("w1", 1, 1), cast_weight(w1_raw[1, 1], nc.scalar.copy, grouped), 1)
        for t in range(PACK):
            for a in range(2):
                for u in range(2):
                    first_pass(a, 1, t, u)
            empty_h(1, t)
        whole, early, late = (0, 0, PAIRS), (1, 0, HALF), (1, HALF, PAIRS)

        def rows_tile(tag, piece, dtype):
            return ring.tile([P, PACK, piece[2] - piece[1]], dtype, name=tag, bufs=1, align_bytes=64)

        def weave_quantize(name, piece, copy):
            src = hs_rows[piece] if name == "hs" else x_rows[piece]
            quantize_act(name, piece[0], interleave(copy, src[:]), piece[1], piece[2])

        hs_rows[whole] = ring.tile([P, PACK, PAIRS], BF16, name="rows_a", bufs=1, align_bytes=64)
        x_rows[whole] = rows_tile("rows_b", whole, BF16)
        for t in range(PACK):
            picked2[whole, t] = ring.tile([P, PAIRS], F32, name="picked", bufs=4)[:]
            pick2(whole, t)
            pick1(whole, t)
        weave_quantize("hs", whole, nc.vector.tensor_copy)
        quantize_weight(("w2", 0, 0), cast_weight(w2_raw[0, 0], nc.scalar.copy), 1)
        w3_sc_raw = ring.tile([P, N], U8, name="w_grouped", bufs=4, align_bytes=64)
        nc.gpsimd.memset(w3_sc_raw[:].bitcast(I32), 0)
        for q in range(4):
            nc.sync.dma_start(
                out=w3_sc_raw[32 * q : 32 * q + 8, :].bitcast(I32),
                in_=w3_scales[:, 4 * q : 4 * q + 4, :].bitcast(I32),
            )
        w3_w = ring.tile([P, 2, N], U16, name="words1", bufs=1, align_bytes=64)
        nc.vector.tensor_copy(
            w3_w[:].rearrange("p b (g t m) -> p (b g) t m", t=PACK, m=P),
            w3_raw[:].bitcast(U16).rearrange("p b (g m t) -> p (b g) t m", t=PACK, m=P),
        )
        w3_sc = [ring.tile([P, N], U8, name="plane", bufs=1, align_bytes=64), held("w3_sc1", [P, N], U8)]
        nc.gpsimd.memset(w3_sc[1][:].bitcast(I32), 0)
        nc.vector.tensor_copy(
            w3_sc[0][:].rearrange("p (g t m) -> p g t m", t=PACK, m=P),
            w3_sc_raw[:].rearrange("p (g m t) -> p g t m", t=PACK, m=P),
        )
        for q in range(4):
            nc.sync.dma_start(
                out=w3_sc[1][32 * q : 32 * q + 4, :].bitcast(I32), in_=w3_sc[0][32 * q + 4 : 32 * q + 8, :].bitcast(I32)
            )
        for t in range(PACK):
            gelu_lift(whole, t)
        weave_quantize("x", whole, nc.scalar.copy)
        quantize_weight(("w2", 1, 0), cast_weight(w2_raw[1, 0], nc.scalar.copy), 1)
        second(("x", "hs"), 0, 0, 0)

        hs_rows[early] = rows_tile("rows_a", early, BF16)
        x_rows[early] = rows_tile("rows_c", early, BF16)
        for t in range(PACK):
            picked2[early, t] = ring.tile([P, HALF], F32, name="picked", bufs=4)[:]
            pick2(early, t)
        for t in range(PACK):
            pick1(early, t)
        for t in range(PACK):
            gelu_lift(early, t)
        weave_quantize("hs", early, nc.vector.tensor_copy)
        weave_quantize("x", early, nc.scalar.copy)
        second(("x", "hs"), 1, 0, 0)
        second(("x", "hs"), 0, 1, 0)
        for b in range(2):
            quantize_weight(("w2", b, 1), cast_weight(w2_raw[b, 1], nc.scalar.copy), 1)
            second(("x", "hs"), b, 0, 1)
        second(("x", "hs"), 0, 1, 1)

        late_picked = rows_tile("rows_b", late, F32)
        hs_rows[late] = rows_tile("rows_c", late, BF16)
        x_rows[late] = rows_tile("rows_d", late, BF16)
        for t in range(PACK):
            picked2[late, t] = late_picked[:, t, :]
            pick2(late, t)
        for t in range(PACK):
            gelu_lift(late, t)
        weave_quantize("x", late, nc.vector.tensor_copy)
        finish(0, 0, False)
        finish(0, 1, False)
        for t in range(PACK):
            pick1(late, t)
        weave_quantize("hs", late, nc.vector.tensor_copy)
        for g in range(2):
            second(("x", "hs"), 1, 1, g)
        for g in range(2):
            finish(1, g, False)
        for q in range(4):
            queue = nc.sync if q % 2 == 0 else nc.scalar
            queue.dma_start(
                out=out_2[:, 4 * q : 4 * q + 4, :].bitcast(I32).rearrange("g r m -> r g m"),
                in_=y_scales[32 * q : 32 * q + 4, :, :].bitcast(I32),
            )
